import numpy as np
CORES = [1,9,17,25,33,41,49,57,65,73,81,89,97,105,113,121,129,137,145,153,161,169,177,185,193,201,209,217,225,233,241,249,257,265,273,281,289,297,305,313,321,329,337,345,353,361,369,377,385,393,401,409,417,425,433,441,449,457,465,473,481,489,497,505]
N = 64
COUNTS = [[(2, 4, 4, 6)[(7 * s + 3 * d) % 4] * (4 if (s // 16 == 1 and d // 16 == 3) else 1) for d in range(N)] for s in range(N)]
XW, YW = 448, 448
def setup_inputs(rng):
    return {"x": rng.standard_normal((N, 128, 448), dtype=np.float32)}
def reference(x):
    y = np.full((N, 128, YW), np.nan, x.dtype)
    fill = [0] * N
    for s in range(N):
        o = 0
        for d in range(N):
            c = COUNTS[s][d]
            y[d][:, fill[d]:fill[d] + c] = x[s][:, o:o + c]
            o += c; fill[d] += c
    return {"y": y}

@@ -1,0 +1,142 @@
+import concourse.bass as bass
+import comms_topo
+
+SCRATCH = {
+    "stage": ("sbuf", [128, 448], "float32"),
+    "land": ("sbuf", [128, 448], "float32"),
+}
+SEMAPHORES = ["loaded", "own", "hand", "relay", "arrived", "stored", "sent"]
+
+PORT_CORES = (2, 3, 6, 7)
+CACHE = {}
+
+
+def core_of(h, k, c):
+    return 128 * h + 8 * k + c
+
+
+def build_plan(counts):
+    n = len(counts)
+    xo = [[sum(counts[s][:d]) for d in range(n + 1)] for s in range(n)]
+    yo = [[sum(counts[t][d] for t in range(s)) for s in range(n + 1)] for d in range(n)]
+    todo = {}
+    fill = {}
+
+    def put(src, stage, dst, soff, doff, w, sem):
+        todo.setdefault(src, {}).setdefault(stage, []).append((dst, soff, doff, w, sem))
+
+    def via(s, mid, dests, sem):
+        src = core_of(s // 16, s % 16, 1)
+        runs = []
+        for d in dests:
+            if d == s:
+                continue
+            if runs and runs[-1][-1] == d - 1:
+                runs[-1].append(d)
+            else:
+                runs.append([d])
+        for run in runs:
+            a, b = xo[s][run[0]], xo[s][run[-1] + 1]
+            at = fill.get(mid, 0)
+            fill[mid] = at + b - a
+            put(src, "load", mid, a, at, b - a, sem)
+            for d in run:
+                put(mid, sem, core_of(d // 16, d % 16, 1), at + xo[s][d] - a, yo[d][s], counts[s][d], "arrived")
+
+    for s in range(n):
+        h, k = s // 16, s % 16
+        sib, cab, dia = h ^ 1, 3 - h, h ^ 2
+        for t in (h, sib):
+            for blk in range(2):
+                die = (blk + k // 8 + (t != h)) % 2
+                c = PORT_CORES[2 * die + (t != h)]
+                via(s, core_of(h, k, c), [16 * t + 8 * blk + i for i in range(8)], "hand")
+        for q in range(4):
+            via(s, core_of(h, k, PORT_CORES[q]), [16 * cab + 4 * q + i for i in range(4)], "hand")
+        if h != 1:
+            seen = [0, 0]
+            for q in range(4):
+                die = (q + k // 4) % 2
+                c = PORT_CORES[2 * die + seen[die]]
+                seen[die] += 1
+                via(s, core_of(cab, k, c), [16 * dia + 4 * q + i for i in range(4)], "relay")
+        else:
+            seen = [0, 0]
+            for q in range(4):
+                die = (q + k // 4) % 2
+                c = PORT_CORES[2 * die + seen[die]]
+                seen[die] += 1
+                for j in range(4 * q, 4 * q + 4):
+                    if (j + k) % 2:
+                        via(s, core_of(cab, k, c), [16 * dia + j], "relay")
+            for j in range(k % 2, 16, 2):
+                c = (0, 4, 5, 4, 5, 4, 5, 0)[k // 2]
+                via(s, core_of(sib, j, c), [16 * dia + j], "relay")
+
+    calls = {}
+    expect = {}
+    for src, stages in todo.items():
+        for stage, ws in stages.items():
+            out = calls.setdefault(src, {}).setdefault(stage, [])
+            for w in sorted(set(x[3] for x in ws)):
+                same = [x for x in ws if x[3] == w]
+                while same:
+                    part, same = same[:8], same[8:]
+                    off = any(x[0] // 8 != src // 8 for x in part)
+                    per = 1
+                    while per * 2 * len(part) <= (8 if off else 16):
+                        per *= 2
+                    call = []
+                    for i, x in enumerate(part):
+                        call.append(x + ((((1 << per) - 1) << (per * i)), per))
+                        e = expect.setdefault(x[0], {})
+                        e[x[4]] = e.get(x[4], 0) + per
+                        e = expect.setdefault(src, {})
+                        e["sent"] = e.get("sent", 0) + per
+                    out.append(call)
+    return {"calls": calls, "expect": expect, "xo": xo, "yo": yo, "fill": fill}
+
+
+def rank_program(g, core, T, topo):
+    if "plan" not in CACHE:
+        CACHE["plan"] = build_plan(T.tables["COUNTS"])
+    plan = CACHE["plan"]
+    calls = plan["calls"].get(core, {})
+    expect = plan["expect"].get(core, {})
+    sems = {"hand": T.sem.hand, "relay": T.sem.relay, "arrived": T.sem.arrived}
+
+    def emit(stage, buf):
+        for call in calls.get(stage, []):
+            trs = []
+            for dst, soff, doff, w, sem, mask, per in call:
+                rid, pid = topo.addr(dst, core)
+                trs.append((rid, pid, soff, doff, w, sems[sem], mask))
+            if len(trs) == 1:
+                rid, pid, soff, doff, w, sem, mask = trs[0]
+                g.remote_dma(T.land[:, doff:doff + w], buf[:, soff:soff + w], sem, T.sem.sent, pid, rid, mask)
+            else:
+                g.remote_dma_fused(
+                    [bass.RemoteDMATransfer(dst_ids=[bass.DstId(rid=rid, pnc=pid)], dma_engine_mask=mask, remote_sem=sem,
+                                            src=buf[:, soff:soff + w], dst=T.land[:, doff:doff + w])
+                     for rid, pid, soff, doff, w, sem, mask in trs],
+                    local_sem=T.sem.sent)
+
+    rank = T.rank_of(core)
+    if rank is None:
+        for stage in ("hand", "relay"):
+            if stage in calls:
+                g.wait_ge(sems[stage], expect[stage])
+                emit(stage, T.land)
+        if "sent" in expect:
+            g.wait_ge(T.sem.sent, expect["sent"])
+        return
+    xo, yo = plan["xo"][rank], plan["yo"][rank]
+    g.dma_start(out=T.stage[:, 0:xo[-1]], in_=T.x[:, 0:xo[-1]]).then_inc(T.sem.loaded, 16)
+    g.dma_start(out=T.land[:, yo[rank]:yo[rank + 1]], in_=T.x[:, xo[rank]:xo[rank + 1]]).then_inc(T.sem.own, 16)
+    g.wait_ge(T.sem.loaded, 16)
+    emit("load", T.stage)
+    g.wait_ge(T.sem.own, 16)
+    g.wait_ge(T.sem.arrived, expect["arrived"])
+    g.dma_start(out=T.y[:, 0:yo[-1]], in_=T.land[:, 0:yo[-1]]).then_inc(T.sem.stored, 16)
+    g.wait_ge(T.sem.stored, 16)
+    g.wait_ge(T.sem.sent, expect["sent"])

@@ -1,5 +1,4 @@
 import concourse.bass as bass
-import comms_topo
 
 SCRATCH = {
     "stage": ("sbuf", [128, 448], "float32"),
@@ -7,12 +6,47 @@ SCRATCH = {
 }
 SEMAPHORES = ["loaded", "own", "hand", "relay", "arrived", "stored", "sent"]
 
-PORT_CORES = (2, 3, 6, 7)
+PORT = ((2, 3), (6, 7))
 CACHE = {}
 
 
 def core_of(h, k, c):
     return 128 * h + 8 * k + c
+
+
+def middlemen(s):
+    h, k = s // 16, s % 16
+    sib, cab, dia = h ^ 1, 3 - h, h ^ 2
+    give = {}
+
+    def add(mid, sem, dests):
+        give.setdefault((mid, sem), []).extend(dests)
+
+    if h == 1:
+        for i, c in enumerate((6, 7, 2, 3)):
+            add(core_of(h, k, c), "hand", range(12 * i, 12 * i + 12))
+    else:
+        for t in (h, sib):
+            for blk in range(2):
+                die = (blk + k // 8 + (t != h)) % 2
+                add(core_of(h, k, PORT[die][t != h]), "hand", range(16 * t + 8 * blk, 16 * t + 8 * blk + 8))
+        for q in range(4):
+            add(core_of(h, k, PORT[q // 2][q % 2]), "hand", range(16 * cab + 4 * q, 16 * cab + 4 * q + 4))
+
+    free = {0: list(PORT[0]), 1: list(PORT[1])}
+    if h == 2:
+        free = {0: [3], 1: [6, 7, 7]}
+    for q in range(4):
+        die = (q + k // 4) % 2
+        if h == 2:
+            die = 0 if q == k // 4 else 1
+        c = free[die].pop(0)
+        add(core_of(cab, k, c), "relay", [16 * dia + j for j in range(4 * q, 4 * q + 4) if h != 1 or (j + k) % 2])
+
+    if h == 1:
+        for j in range(k % 2, 16, 2):
+            add(core_of(sib, j, (0, 4, 5, 4, 5, 4, 5, 0)[k // 2]), "relay", [16 * dia + j])
+    return give
 
 
 def build_plan(counts):
@@ -22,77 +56,48 @@ def build_plan(counts):
     todo = {}
     fill = {}
 
-    def put(src, stage, dst, soff, doff, w, sem):
-        todo.setdefault(src, {}).setdefault(stage, []).append((dst, soff, doff, w, sem))
-
-    def via(s, mid, dests, sem):
-        src = core_of(s // 16, s % 16, 1)
-        runs = []
-        for d in dests:
-            if d == s:
-                continue
-            if runs and runs[-1][-1] == d - 1:
-                runs[-1].append(d)
-            else:
-                runs.append([d])
-        for run in runs:
-            a, b = xo[s][run[0]], xo[s][run[-1] + 1]
-            at = fill.get(mid, 0)
-            fill[mid] = at + b - a
-            put(src, "load", mid, a, at, b - a, sem)
-            for d in run:
-                put(mid, sem, core_of(d // 16, d % 16, 1), at + xo[s][d] - a, yo[d][s], counts[s][d], "arrived")
+    def put(src, after, dst, soff, doff, w, sem):
+        todo.setdefault(src, {}).setdefault(after, []).append((dst, soff, doff, w, sem))
 
     for s in range(n):
-        h, k = s // 16, s % 16
-        sib, cab, dia = h ^ 1, 3 - h, h ^ 2
-        for t in (h, sib):
-            for blk in range(2):
-                die = (blk + k // 8 + (t != h)) % 2
-                c = PORT_CORES[2 * die + (t != h)]
-                via(s, core_of(h, k, c), [16 * t + 8 * blk + i for i in range(8)], "hand")
-        for q in range(4):
-            via(s, core_of(h, k, PORT_CORES[q]), [16 * cab + 4 * q + i for i in range(4)], "hand")
-        if h != 1:
-            seen = [0, 0]
-            for q in range(4):
-                die = (q + k // 4) % 2
-                c = PORT_CORES[2 * die + seen[die]]
-                seen[die] += 1
-                via(s, core_of(cab, k, c), [16 * dia + 4 * q + i for i in range(4)], "relay")
-        else:
-            seen = [0, 0]
-            for q in range(4):
-                die = (q + k // 4) % 2
-                c = PORT_CORES[2 * die + seen[die]]
-                seen[die] += 1
-                for j in range(4 * q, 4 * q + 4):
-                    if (j + k) % 2:
-                        via(s, core_of(cab, k, c), [16 * dia + j], "relay")
-            for j in range(k % 2, 16, 2):
-                c = (0, 4, 5, 4, 5, 4, 5, 0)[k // 2]
-                via(s, core_of(sib, j, c), [16 * dia + j], "relay")
+        src = core_of(s // 16, s % 16, 1)
+        for (mid, sem), dests in middlemen(s).items():
+            runs = []
+            for d in sorted(dests):
+                if d == s:
+                    continue
+                if runs and runs[-1][-1] == d - 1:
+                    runs[-1].append(d)
+                else:
+                    runs.append([d])
+            for run in runs:
+                a, b = xo[s][run[0]], xo[s][run[-1] + 1]
+                at = fill.get(mid, 0)
+                fill[mid] = at + b - a
+                put(src, "load", mid, a, at, b - a, sem)
+                for d in run:
+                    put(mid, sem, core_of(d // 16, d % 16, 1), at + xo[s][d] - a, yo[d][s], counts[s][d], "arrived")
 
     calls = {}
     expect = {}
     for src, stages in todo.items():
-        for stage, ws in stages.items():
-            out = calls.setdefault(src, {}).setdefault(stage, [])
+        for after, ws in stages.items():
+            out = calls.setdefault(src, {}).setdefault(after, [])
             for w in sorted(set(x[3] for x in ws)):
-                same = [x for x in ws if x[3] == w]
-                while same:
-                    part, same = same[:8], same[8:]
-                    off = any(x[0] // 8 != src // 8 for x in part)
-                    per = 1
-                    while per * 2 * len(part) <= (8 if off else 16):
-                        per *= 2
+                far = [x for x in ws if x[3] == w and x[0] // 8 != src // 8]
+                near = [x for x in ws if x[3] == w and x[0] // 8 == src // 8]
+                while far or near:
                     call = []
-                    for i, x in enumerate(part):
-                        call.append(x + ((((1 << per) - 1) << (per * i)), per))
-                        e = expect.setdefault(x[0], {})
-                        e[x[4]] = e.get(x[4], 0) + per
-                        e = expect.setdefault(src, {})
-                        e["sent"] = e.get("sent", 0) + per
+                    for part, first, room in ((far[:8], 0, 8), (near[:8], 8 if far else 0, 8 if far else 16)):
+                        per = 1
+                        while part and per * 2 * len(part) <= room:
+                            per *= 2
+                        for i, x in enumerate(part):
+                            call.append(x + (((1 << per) - 1) << (first + per * i),))
+                            for core, sem in ((x[0], x[4]), (src, "sent")):
+                                e = expect.setdefault(core, {})
+                                e[sem] = e.get(sem, 0) + per
+                    far, near = far[8:], near[8:]
                     out.append(call)
     return {"calls": calls, "expect": expect, "xo": xo, "yo": yo, "fill": fill}
 
@@ -105,31 +110,31 @@ def rank_program(g, core, T, topo):
     expect = plan["expect"].get(core, {})
     sems = {"hand": T.sem.hand, "relay": T.sem.relay, "arrived": T.sem.arrived}
 
-    def emit(stage, buf):
-        for call in calls.get(stage, []):
-            trs = []
-            for dst, soff, doff, w, sem, mask, per in call:
+    def emit(after, buf):
+        for call in calls.get(after, []):
+            if len(call) == 1:
+                dst, soff, doff, w, sem, mask = call[0]
                 rid, pid = topo.addr(dst, core)
-                trs.append((rid, pid, soff, doff, w, sems[sem], mask))
-            if len(trs) == 1:
-                rid, pid, soff, doff, w, sem, mask = trs[0]
-                g.remote_dma(T.land[:, doff:doff + w], buf[:, soff:soff + w], sem, T.sem.sent, pid, rid, mask)
-            else:
-                g.remote_dma_fused(
-                    [bass.RemoteDMATransfer(dst_ids=[bass.DstId(rid=rid, pnc=pid)], dma_engine_mask=mask, remote_sem=sem,
-                                            src=buf[:, soff:soff + w], dst=T.land[:, doff:doff + w])
-                     for rid, pid, soff, doff, w, sem, mask in trs],
-                    local_sem=T.sem.sent)
+                g.remote_dma(T.land[:, doff:doff + w], buf[:, soff:soff + w], sems[sem], T.sem.sent, pid, rid, mask)
+                continue
+            trs = []
+            for dst, soff, doff, w, sem, mask in call:
+                rid, pid = topo.addr(dst, core)
+                trs.append(bass.RemoteDMATransfer(dst_ids=[bass.DstId(rid=rid, pnc=pid)], dma_engine_mask=mask,
+                                                  remote_sem=sems[sem], src=buf[:, soff:soff + w],
+                                                  dst=T.land[:, doff:doff + w]))
+            g.remote_dma_fused(trs, local_sem=T.sem.sent)
 
     rank = T.rank_of(core)
     if rank is None:
-        for stage in ("hand", "relay"):
-            if stage in calls:
-                g.wait_ge(sems[stage], expect[stage])
-                emit(stage, T.land)
+        for after in ("hand", "relay"):
+            if after in calls:
+                g.wait_ge(sems[after], expect[after])
+                emit(after, T.land)
         if "sent" in expect:
             g.wait_ge(T.sem.sent, expect["sent"])
         return
+
     xo, yo = plan["xo"][rank], plan["yo"][rank]
     g.dma_start(out=T.stage[:, 0:xo[-1]], in_=T.x[:, 0:xo[-1]]).then_inc(T.sem.loaded, 16)
     g.dma_start(out=T.land[:, yo[rank]:yo[rank + 1]], in_=T.x[:, xo[rank]:xo[rank + 1]]).then_inc(T.sem.own, 16)

@@ -7,6 +7,8 @@ SCRATCH = {
 SEMAPHORES = ["loaded", "own", "hand", "relay", "arrived", "stored", "sent"]
 
 PORT = ((2, 3), (6, 7))
+CABLE_FIRST = (1, 3, 4, 7)
+RACK_FIRST = (0, 2, 5, 6)
 CACHE = {}
 
 
@@ -14,39 +16,12 @@ def core_of(h, k, c):
     return 128 * h + 8 * k + c
 
 
-def middlemen(s):
-    h, k = s // 16, s % 16
-    sib, cab, dia = h ^ 1, 3 - h, h ^ 2
-    give = {}
+def rank_core(r):
+    return core_of(r // 16, r % 16, 1)
 
-    def add(mid, sem, dests):
-        give.setdefault((mid, sem), []).extend(dests)
 
-    if h == 1:
-        for i, c in enumerate((6, 7, 2, 3)):
-            add(core_of(h, k, c), "hand", range(12 * i, 12 * i + 12))
-    else:
-        for t in (h, sib):
-            for blk in range(2):
-                die = (blk + k // 8 + (t != h)) % 2
-                add(core_of(h, k, PORT[die][t != h]), "hand", range(16 * t + 8 * blk, 16 * t + 8 * blk + 8))
-        for q in range(4):
-            add(core_of(h, k, PORT[q // 2][q % 2]), "hand", range(16 * cab + 4 * q, 16 * cab + 4 * q + 4))
-
-    free = {0: list(PORT[0]), 1: list(PORT[1])}
-    if h == 2:
-        free = {0: [3], 1: [6, 7, 7]}
-    for q in range(4):
-        die = (q + k // 4) % 2
-        if h == 2:
-            die = 0 if q == k // 4 else 1
-        c = free[die].pop(0)
-        add(core_of(cab, k, c), "relay", [16 * dia + j for j in range(4 * q, 4 * q + 4) if h != 1 or (j + k) % 2])
-
-    if h == 1:
-        for j in range(k % 2, 16, 2):
-            add(core_of(sib, j, (0, 4, 5, 4, 5, 4, 5, 0)[k // 2]), "relay", [16 * dia + j])
-    return give
+def shift(h, m):
+    return 1 if m % 2 and (m % 4 == 3) != (h == 0) else 0
 
 
 def build_plan(counts):
@@ -55,49 +30,94 @@ def build_plan(counts):
     yo = [[sum(counts[t][d] for t in range(s)) for s in range(n + 1)] for d in range(n)]
     todo = {}
     fill = {}
+    slot = {}
 
     def put(src, after, dst, soff, doff, w, sem):
         todo.setdefault(src, {}).setdefault(after, []).append((dst, soff, doff, w, sem))
 
-    for s in range(n):
-        src = core_of(s // 16, s % 16, 1)
-        for (mid, sem), dests in middlemen(s).items():
-            runs = []
-            for d in sorted(dests):
-                if d == s:
-                    continue
-                if runs and runs[-1][-1] == d - 1:
-                    runs[-1].append(d)
-                else:
-                    runs.append([d])
-            for run in runs:
-                a, b = xo[s][run[0]], xo[s][run[-1] + 1]
-                at = fill.get(mid, 0)
-                fill[mid] = at + b - a
-                put(src, "load", mid, a, at, b - a, sem)
+    def room(core, w):
+        at = fill.get(core, 0)
+        fill[core] = at + w
+        return at
+
+    def hold(s, mid, dests):
+        if mid == rank_core(s):
+            return "load", {d: xo[s][d] for d in dests}
+        col = {}
+        for run in ([d for d in dests if d < s], [d for d in dests if d > s]):
+            if run:
+                a, w = xo[s][run[0]], xo[s][run[-1] + 1] - xo[s][run[0]]
+                at = room(mid, w)
+                put(rank_core(s), "load", mid, a, at, w, "hand")
                 for d in run:
-                    put(mid, sem, core_of(d // 16, d % 16, 1), at + xo[s][d] - a, yo[d][s], counts[s][d], "arrived")
+                    col[d] = at + xo[s][d] - a
+        return "hand", col
+
+    for s in range(n):
+        h, k = s // 16, s % 16
+        sib, cab, dia = h ^ 1, 3 - h, h ^ 2
+        b = k // 8
+
+        i, s0 = (k % 8) // 2, s - s % 2
+        for q in (2 - 2 * b, 3 - 2 * b):
+            mid = core_of(h, k, PORT[(q + k // 4) % 2][0])
+            after, col = hold(s, mid, list(range(16 * dia + 4 * q, 16 * dia + 4 * q + 4)))
+            for d in col:
+                j = d % 16
+                via = core_of(sib, j, RACK_FIRST[(i - 1 - shift(sib, j)) % 4])
+                if (d, i) not in slot:
+                    w = counts[s0][d] + counts[s0 + 1][d]
+                    slot[(d, i)] = room(via, w)
+                    put(via, "relay", rank_core(d), slot[(d, i)], yo[d][s0], w, "arrived")
+                put(mid, after, via, col[d], slot[(d, i)] + yo[d][s] - yo[d][s0], counts[s][d], "relay")
+
+        for p in range(4):
+            mid = core_of(h, k, CABLE_FIRST[(p - shift(h, k)) % 4])
+            d0 = 16 * dia + 8 * b + 2 * p
+            after, col = hold(s, mid, [d0, d0 + 1])
+            via = core_of(cab, k, PORT[(2 * b + p // 2 + k // 4) % 2][1])
+            w = counts[s][d0] + counts[s][d0 + 1]
+            at = room(via, w)
+            put(mid, after, via, col[d0], at, w, "relay")
+            for d in (d0, d0 + 1):
+                put(via, "relay", rank_core(d), at + xo[s][d] - xo[s][d0], yo[d][s], counts[s][d], "arrived")
+
+        def straight(mid, first, count):
+            after, col = hold(s, mid, list(range(first, first + count)))
+            for d in col:
+                put(mid, after, rank_core(d), col[d], yo[d][s], counts[s][d], "arrived")
+
+        for die in range(2):
+            straight(core_of(h, k, PORT[die][1]), 16 * h + 8 * ((b + die) % 2), 8)
+            straight(core_of(h, k, PORT[die][0]), 16 * sib + 8 * ((b + die + 1) % 2), 8)
+        for q in range(4):
+            straight(core_of(h, k, PORT[q // 2][q % 2]), 16 * cab + 4 * q, 4)
 
     calls = {}
     expect = {}
     for src, stages in todo.items():
         for after, ws in stages.items():
             out = calls.setdefault(src, {}).setdefault(after, [])
-            for w in sorted(set(x[3] for x in ws)):
+            widths = []
+            for x in ws:
+                if x[3] not in widths:
+                    widths.append(x[3])
+            for w in widths:
                 far = [x for x in ws if x[3] == w and x[0] // 8 != src // 8]
                 near = [x for x in ws if x[3] == w and x[0] // 8 == src // 8]
                 while far or near:
                     call = []
-                    for part, first, room in ((far[:8], 0, 8), (near[:8], 8 if far else 0, 8 if far else 16)):
+                    lo, hi = (8, 8) if far else (0, 16)
+                    for part, first, engines in ((far[:8], 0, 8), (near[:hi], lo, hi)):
                         per = 1
-                        while part and per * 2 * len(part) <= room:
+                        while part and per * 2 * len(part) <= engines:
                             per *= 2
                         for i, x in enumerate(part):
                             call.append(x + (((1 << per) - 1) << (first + per * i),))
                             for core, sem in ((x[0], x[4]), (src, "sent")):
                                 e = expect.setdefault(core, {})
                                 e[sem] = e.get(sem, 0) + per
-                    far, near = far[8:], near[8:]
+                    far, near = far[8:], near[hi:]
                     out.append(call)
     return {"calls": calls, "expect": expect, "xo": xo, "yo": yo, "fill": fill}
 

import concourse.bass as bass

SCRATCH = {
    "stage": ("sbuf", [128, 448], "float32"),
    "land": ("sbuf", [128, 448], "float32"),
}
SEMAPHORES = ["loaded", "own", "hand", "relay", "arrived", "stored", "sent"]

PORT = ((2, 3), (6, 7))
CABLE_FIRST = (1, 3, 4, 7)
RACK_FIRST = (0, 2, 5, 6)
CACHE = {}


def core_of(h, k, c):
    return 128 * h + 8 * k + c


def rank_core(r):
    return core_of(r // 16, r % 16, 1)


def shift(h, m):
    return 1 if m % 2 and (m % 4 == 3) != (h == 0) else 0


def build_plan(counts):
    n = len(counts)
    xo = [[sum(counts[s][:d]) for d in range(n + 1)] for s in range(n)]
    yo = [[sum(counts[t][d] for t in range(s)) for s in range(n + 1)] for d in range(n)]
    todo = {}
    fill = {}
    slot = {}

    def put(src, after, dst, soff, doff, w, sem):
        todo.setdefault(src, {}).setdefault(after, []).append((dst, soff, doff, w, sem))

    def room(core, w):
        at = fill.get(core, 0)
        fill[core] = at + w
        return at

    def hold(s, mid, dests):
        if mid == rank_core(s):
            return "load", {d: xo[s][d] for d in dests}
        col = {}
        for run in ([d for d in dests if d < s], [d for d in dests if d > s]):
            if run:
                a, w = xo[s][run[0]], xo[s][run[-1] + 1] - xo[s][run[0]]
                at = room(mid, w)
                put(rank_core(s), "load", mid, a, at, w, "hand")
                for d in run:
                    col[d] = at + xo[s][d] - a
        return "hand", col

    for s in range(n):
        h, k = s // 16, s % 16
        sib, cab, dia = h ^ 1, 3 - h, h ^ 2
        b = k // 8

        i, s0 = (k % 8) // 2, s - s % 2
        for q in (2 - 2 * b, 3 - 2 * b):
            mid = core_of(h, k, PORT[(q + k // 4) % 2][0])
            after, col = hold(s, mid, list(range(16 * dia + 4 * q, 16 * dia + 4 * q + 4)))
            for d in col:
                j = d % 16
                via = core_of(sib, j, RACK_FIRST[(i - 1 - shift(sib, j)) % 4])
                if (d, i) not in slot:
                    w = counts[s0][d] + counts[s0 + 1][d]
                    slot[(d, i)] = room(via, w)
                    put(via, "relay", rank_core(d), slot[(d, i)], yo[d][s0], w, "arrived")
                put(mid, after, via, col[d], slot[(d, i)] + yo[d][s] - yo[d][s0], counts[s][d], "relay")

        for p in range(4):
            mid = core_of(h, k, CABLE_FIRST[(p - shift(h, k)) % 4])
            d0 = 16 * dia + 8 * b + 2 * p
            after, col = hold(s, mid, [d0, d0 + 1])
            via = core_of(cab, k, PORT[(2 * b + p // 2 + k // 4) % 2][1])
            w = counts[s][d0] + counts[s][d0 + 1]
            at = room(via, w)
            put(mid, after, via, col[d0], at, w, "relay")
            for d in (d0, d0 + 1):
                put(via, "relay", rank_core(d), at + xo[s][d] - xo[s][d0], yo[d][s], counts[s][d], "arrived")

        def straight(mid, first, count):
            after, col = hold(s, mid, list(range(first, first + count)))
            for d in col:
                put(mid, after, rank_core(d), col[d], yo[d][s], counts[s][d], "arrived")

        for die in range(2):
            straight(core_of(h, k, PORT[die][1]), 16 * h + 8 * ((b + die) % 2), 8)
            straight(core_of(h, k, PORT[die][0]), 16 * sib + 8 * ((b + die + 1) % 2), 8)
        for q in range(4):
            straight(core_of(h, k, PORT[q // 2][q % 2]), 16 * cab + 4 * q, 4)

    calls = {}
    expect = {}
    for src, stages in todo.items():
        for after, ws in stages.items():
            out = calls.setdefault(src, {}).setdefault(after, [])
            widths = []
            for x in ws:
                if x[3] not in widths:
                    widths.append(x[3])
            for w in widths:
                far = [x for x in ws if x[3] == w and x[0] // 8 != src // 8]
                near = [x for x in ws if x[3] == w and x[0] // 8 == src // 8]
                while far or near:
                    call = []
                    lo, hi = (8, 8) if far else (0, 16)
                    for part, first, engines in ((far[:8], 0, 8), (near[:hi], lo, hi)):
                        per = 1
                        while part and per * 2 * len(part) <= engines:
                            per *= 2
                        for i, x in enumerate(part):
                            call.append(x + (((1 << per) - 1) << (first + per * i),))
                            for core, sem in ((x[0], x[4]), (src, "sent")):
                                e = expect.setdefault(core, {})
                                e[sem] = e.get(sem, 0) + per
                    far, near = far[8:], near[hi:]
                    out.append(call)
    return {"calls": calls, "expect": expect, "xo": xo, "yo": yo, "fill": fill}


def rank_program(g, core, T, topo):
    if "plan" not in CACHE:
        CACHE["plan"] = build_plan(T.tables["COUNTS"])
    plan = CACHE["plan"]
    calls = plan["calls"].get(core, {})
    expect = plan["expect"].get(core, {})
    sems = {"hand": T.sem.hand, "relay": T.sem.relay, "arrived": T.sem.arrived}

    def emit(after, buf):
        for call in calls.get(after, []):
            if len(call) == 1:
                dst, soff, doff, w, sem, mask = call[0]
                rid, pid = topo.addr(dst, core)
                g.remote_dma(T.land[:, doff:doff + w], buf[:, soff:soff + w], sems[sem], T.sem.sent, pid, rid, mask)
                continue
            trs = []
            for dst, soff, doff, w, sem, mask in call:
                rid, pid = topo.addr(dst, core)
                trs.append(bass.RemoteDMATransfer(dst_ids=[bass.DstId(rid=rid, pnc=pid)], dma_engine_mask=mask,
                                                  remote_sem=sems[sem], src=buf[:, soff:soff + w],
                                                  dst=T.land[:, doff:doff + w]))
            g.remote_dma_fused(trs, local_sem=T.sem.sent)

    rank = T.rank_of(core)
    if rank is None:
        for after in ("hand", "relay"):
            if after in calls:
                g.wait_ge(sems[after], expect[after])
                emit(after, T.land)
        if "sent" in expect:
            g.wait_ge(T.sem.sent, expect["sent"])
        return

    xo, yo = plan["xo"][rank], plan["yo"][rank]
    g.dma_start(out=T.stage[:, 0:xo[-1]], in_=T.x[:, 0:xo[-1]]).then_inc(T.sem.loaded, 16)
    g.dma_start(out=T.land[:, yo[rank]:yo[rank + 1]], in_=T.x[:, xo[rank]:xo[rank + 1]]).then_inc(T.sem.own, 16)
    g.wait_ge(T.sem.loaded, 16)
    emit("load", T.stage)
    g.wait_ge(T.sem.own, 16)
    g.wait_ge(T.sem.arrived, expect["arrived"])
    g.dma_start(out=T.y[:, 0:yo[-1]], in_=T.land[:, 0:yo[-1]]).then_inc(T.sem.stored, 16)
    g.wait_ge(T.sem.stored, 16)
    g.wait_ge(T.sem.sent, expect["sent"])
